import numpy as np
CORES = [1,7,41,47,81,87,121,127]
N = 8
def setup_inputs(rng):
    return {"x": rng.standard_normal((N, 128, 384), dtype=np.float32)}
def reference(x):
    s = x.sum(axis=0, dtype=np.float64).astype(x.dtype)
    b = 384 // N
    return {"y": np.stack([s[:, r * b:(r + 1) * b] for r in range(N)])}

@@ -1,0 +1,100 @@
+from concourse.bass import DstId, RemoteDMATransfer
+from concourse.mybir import AluOpType
+
+RING = [1, 7, 47, 41, 121, 127, 87, 81]
+NSL = 8
+ROWS = 16
+B = 48
+
+SCRATCH = {
+    "L": ("dram", [6, 128, 6], "float32"),
+    "S": ("dram", [4, 128, 6], "float32"),
+}
+SEMAPHORES = ["G0", "G1", "go", "acc"]
+
+
+def _plan():
+    steps = []
+    for k in range(NSL):
+        H = 4 if k % 2 == 0 else 3
+        for h in range(1, H + 1):
+            steps.append((h, H, k, (k + 1) % NSL))
+    return steps
+
+
+def rank_program(g, core, T, topo):
+    if T.rank_of(core) is None:
+        return
+    p = RING.index(core)
+    me = T.rank_of(core)
+    steps = _plan()
+    NS = len(steps)
+    G = [T.sem.G0, T.sem.G1]
+    cum = [0, 0]
+    nbr = [RING[(p + 1) % 8], RING[(p - 1) % 8]]
+    ids, masks = [], []
+    for d in range(2):
+        rid, pid, _se = topo.addr(nbr[d])
+        ids.append(DstId(rid=rid, pnc=pid))
+        masks.append(0xFF00 if topo.chip(nbr[d]) == topo.chip(core) else 0x00FF)
+    lq = [g.sync, g.scalar]
+
+    def load(n):
+        h, H, s0, s1 = steps[n]
+        for d in range(2):
+            q = (p + (H - h + 1)) % 8 if d == 0 else (p - (H - h + 1)) % 8
+            b = T.rank_of(RING[q])
+            s = s0 if d == 0 else s1
+            lq[d].dma_start(T.S[2 * (n % 2) + d],
+                            T.x[ROWS * s:ROWS * (s + 1), B * b:B * (b + 1)]).then_inc(G[n % 2], 16)
+
+    load(0)
+    load(1)
+    g.scalar.dma_start(T.y[:, :], T.x[:, B * me:B * (me + 1)]).then_inc(G[1], 16)
+
+    acc = 0
+    for n in range(NS + 1):
+        add = 0
+        if n < NS:
+            add += 32
+        if n >= 1:
+            add += 32
+        if n == 1:
+            add += 16
+        cum[n % 2] += add
+        g.wait_ge(G[n % 2], cum[n % 2])
+        if acc:
+            g.wait_ge(T.sem.acc, acc)
+        if 1 <= n and n + 1 < NS:
+            g.sem_inc(T.sem.go, 1)
+            for d in range(2):
+                lq[d].wait_ge(T.sem.go, n)
+            load(n + 1)
+        if n < NS:
+            h, H, s0, s1 = steps[n]
+            trs = []
+            for d in range(2):
+                S = T.S[2 * (n % 2) + d]
+                dst = T.L[2 * (n % 3) + d]
+                if h == 1:
+                    trs.append(RemoteDMATransfer(dst_ids=[ids[d]], dma_engine_mask=masks[d], remote_sem=G[(n + 1) % 2],
+                                                 src=S, dst=dst, alu_op=0))
+                else:
+                    trs.append(RemoteDMATransfer(dst_ids=[ids[d]], dma_engine_mask=masks[d], remote_sem=G[(n + 1) % 2],
+                                                 srcs=[T.L[2 * ((n - 1) % 3) + d], S], dsts=[dst], alu_op=1))
+            g.remote_dma_fused(trs, local_sem=G[(n + 1) % 2])
+        if n >= 1:
+            h, H, s0, s1 = steps[n - 1]
+            if h == H:
+                r = 2 * ((n - 1) % 3)
+                if s1 == s0 + 1:
+                    g.dma_start(T.y[ROWS * s0:ROWS * (s0 + 2), :], T.L[r:r + 2],
+                                accum_op=AluOpType.add).then_inc(T.sem.acc, 16)
+                    acc += 16
+                else:
+                    g.dma_start(T.y[ROWS * s0:ROWS * (s0 + 1), :], T.L[r],
+                                accum_op=AluOpType.add).then_inc(T.sem.acc, 16)
+                    g.dma_start(T.y[ROWS * s1:ROWS * (s1 + 1), :], T.L[r + 1],
+                                accum_op=AluOpType.add).then_inc(T.sem.acc, 16)
+                    acc += 32
+    g.wait_ge(T.sem.acc, acc)

@@ -37,11 +37,12 @@ def rank_program(g, core, T, topo):
         rid, pid, _se = topo.addr(nbr[d])
         ids.append(DstId(rid=rid, pnc=pid))
         masks.append(0xFF00 if topo.chip(nbr[d]) == topo.chip(core) else 0x00FF)
+    order = [0, 1] if masks[0] == 0x00FF else [1, 0]
     lq = [g.sync, g.scalar]
 
     def load(n):
         h, H, s0, s1 = steps[n]
-        for d in range(2):
+        for d in order:
             q = (p + (H - h + 1)) % 8 if d == 0 else (p - (H - h + 1)) % 8
             b = T.rank_of(RING[q])
             s = s0 if d == 0 else s1
@@ -73,7 +74,7 @@ def rank_program(g, core, T, topo):
         if n < NS:
             h, H, s0, s1 = steps[n]
             trs = []
-            for d in range(2):
+            for d in order:
                 S = T.S[2 * (n % 2) + d]
                 dst = T.L[2 * (n % 3) + d]
                 if h == 1:

@@ -2,15 +2,14 @@ from concourse.bass import DstId, RemoteDMATransfer
 from concourse.mybir import AluOpType
 
 RING = [1, 7, 47, 41, 121, 127, 87, 81]
-NSL = 8
-ROWS = 16
+NSL = 6
 B = 48
 
 SCRATCH = {
-    "L": ("dram", [6, 128, 6], "float32"),
-    "S": ("dram", [4, 128, 6], "float32"),
+    "L": ("dram", [6, 128, 8], "float32"),
+    "S": ("dram", [2, 128, 8], "float32"),
 }
-SEMAPHORES = ["G0", "G1", "go", "acc"]
+SEMAPHORES = ["G0", "G1", "left", "acc"]
 
 
 def _plan():
@@ -40,17 +39,20 @@ def rank_program(g, core, T, topo):
     order = [0, 1] if masks[0] == 0x00FF else [1, 0]
     lq = [g.sync, g.scalar]
 
+    def piece(t, s, c0):
+        r0, c = 64 * (s // 3), c0 + 16 * (s % 3)
+        return t[r0:r0 + 64, c:c + 16]
+
     def load(n):
         h, H, s0, s1 = steps[n]
         for d in order:
             q = (p + (H - h + 1)) % 8 if d == 0 else (p - (H - h + 1)) % 8
             b = T.rank_of(RING[q])
-            s = s0 if d == 0 else s1
-            lq[d].dma_start(T.S[2 * (n % 2) + d],
-                            T.x[ROWS * s:ROWS * (s + 1), B * b:B * (b + 1)]).then_inc(G[n % 2], 16)
+            if n >= 1:
+                lq[d].wait_ge(T.sem.left, 16 * n)
+            lq[d].dma_start(T.S[d], piece(T.x, s0 if d == 0 else s1, B * b)).then_inc(G[n % 2], 16)
 
     load(0)
-    load(1)
     g.scalar.dma_start(T.y[:, :], T.x[:, B * me:B * (me + 1)]).then_inc(G[1], 16)
 
     acc = 0
@@ -59,43 +61,33 @@ def rank_program(g, core, T, topo):
         if n < NS:
             add += 32
         if n >= 1:
-            add += 32
+            add += 16
         if n == 1:
             add += 16
         cum[n % 2] += add
         g.wait_ge(G[n % 2], cum[n % 2])
         if acc:
             g.wait_ge(T.sem.acc, acc)
-        if 1 <= n and n + 1 < NS:
-            g.sem_inc(T.sem.go, 1)
-            for d in range(2):
-                lq[d].wait_ge(T.sem.go, n)
-            load(n + 1)
         if n < NS:
             h, H, s0, s1 = steps[n]
             trs = []
             for d in order:
-                S = T.S[2 * (n % 2) + d]
                 dst = T.L[2 * (n % 3) + d]
                 if h == 1:
                     trs.append(RemoteDMATransfer(dst_ids=[ids[d]], dma_engine_mask=masks[d], remote_sem=G[(n + 1) % 2],
-                                                 src=S, dst=dst, alu_op=0))
+                                                 src=T.S[d], dst=dst, alu_op=0))
                 else:
                     trs.append(RemoteDMATransfer(dst_ids=[ids[d]], dma_engine_mask=masks[d], remote_sem=G[(n + 1) % 2],
-                                                 srcs=[T.L[2 * ((n - 1) % 3) + d], S], dsts=[dst], alu_op=1))
-            g.remote_dma_fused(trs, local_sem=G[(n + 1) % 2])
+                                                 srcs=[T.L[2 * ((n - 1) % 3) + d], T.S[d]], dsts=[dst], alu_op=1))
+            g.remote_dma_fused(trs, local_sem=T.sem.left)
+            if n + 1 < NS:
+                load(n + 1)
         if n >= 1:
             h, H, s0, s1 = steps[n - 1]
             if h == H:
                 r = 2 * ((n - 1) % 3)
-                if s1 == s0 + 1:
-                    g.dma_start(T.y[ROWS * s0:ROWS * (s0 + 2), :], T.L[r:r + 2],
-                                accum_op=AluOpType.add).then_inc(T.sem.acc, 16)
-                    acc += 16
-                else:
-                    g.dma_start(T.y[ROWS * s0:ROWS * (s0 + 1), :], T.L[r],
-                                accum_op=AluOpType.add).then_inc(T.sem.acc, 16)
-                    g.dma_start(T.y[ROWS * s1:ROWS * (s1 + 1), :], T.L[r + 1],
-                                accum_op=AluOpType.add).then_inc(T.sem.acc, 16)
-                    acc += 32
+                g.dma_start(piece(T.y, s0, 0), T.L[r], accum_op=AluOpType.add).then_inc(T.sem.acc, 16)
+                g.dma_start(piece(T.y, s1, 0), T.L[r + 1], accum_op=AluOpType.add).then_inc(T.sem.acc, 16)
+                acc += 32
+    g.wait_ge(T.sem.left, 16 * NS)
     g.wait_ge(T.sem.acc, acc)

@@ -39,9 +39,10 @@ def rank_program(g, core, T, topo):
     order = [0, 1] if masks[0] == 0x00FF else [1, 0]
     lq = [g.sync, g.scalar]
 
-    def piece(t, s, c0):
-        r0, c = 64 * (s // 3), c0 + 16 * (s % 3)
-        return t[r0:r0 + 64, c:c + 16]
+    def piece(t, s, c0, m=1):
+        if s < 4:
+            return t[32 * s:32 * (s + m), c0:c0 + 32]
+        return t[64 * (s - 4):64 * (s - 4 + m), c0 + 32:c0 + 48]
 
     def load(n):
         h, H, s0, s1 = steps[n]
@@ -86,8 +87,12 @@ def rank_program(g, core, T, topo):
             h, H, s0, s1 = steps[n - 1]
             if h == H:
                 r = 2 * ((n - 1) % 3)
-                g.dma_start(piece(T.y, s0, 0), T.L[r], accum_op=AluOpType.add).then_inc(T.sem.acc, 16)
-                g.dma_start(piece(T.y, s1, 0), T.L[r + 1], accum_op=AluOpType.add).then_inc(T.sem.acc, 16)
-                acc += 32
+                if s0 in (0, 1, 2, 4):
+                    g.dma_start(piece(T.y, s0, 0, 2), T.L[r:r + 2], accum_op=AluOpType.add).then_inc(T.sem.acc, 16)
+                    acc += 16
+                else:
+                    g.dma_start(piece(T.y, s0, 0), T.L[r], accum_op=AluOpType.add).then_inc(T.sem.acc, 16)
+                    g.dma_start(piece(T.y, s1, 0), T.L[r + 1], accum_op=AluOpType.add).then_inc(T.sem.acc, 16)
+                    acc += 32
     g.wait_ge(T.sem.left, 16 * NS)
     g.wait_ge(T.sem.acc, acc)

@@ -6,10 +6,9 @@ NSL = 6
 B = 48
 
 SCRATCH = {
-    "L": ("dram", [6, 128, 8], "float32"),
-    "S": ("dram", [2, 128, 8], "float32"),
+    "L": ("dram", [8, 128, 8], "float32"),
 }
-SEMAPHORES = ["G0", "G1", "left", "acc"]
+SEMAPHORES = ["G0", "G1", "go", "acc"]
 
 
 def _plan():
@@ -44,16 +43,18 @@ def rank_program(g, core, T, topo):
             return t[32 * s:32 * (s + m), c0:c0 + 32]
         return t[64 * (s - 4):64 * (s - 4 + m), c0 + 32:c0 + 48]
 
+    def stage(n, d):
+        return T.L[2 * ((n + 1) % 4) + (1 - d)]
+
     def load(n):
         h, H, s0, s1 = steps[n]
         for d in order:
             q = (p + (H - h + 1)) % 8 if d == 0 else (p - (H - h + 1)) % 8
             b = T.rank_of(RING[q])
-            if n >= 1:
-                lq[d].wait_ge(T.sem.left, 16 * n)
-            lq[d].dma_start(T.S[d], piece(T.x, s0 if d == 0 else s1, B * b)).then_inc(G[n % 2], 16)
+            lq[d].dma_start(stage(n, d), piece(T.x, s0 if d == 0 else s1, B * b)).then_inc(G[n % 2], 16)
 
     load(0)
+    load(1)
     g.scalar.dma_start(T.y[:, :], T.x[:, B * me:B * (me + 1)]).then_inc(G[1], 16)
 
     acc = 0
@@ -62,31 +63,34 @@ def rank_program(g, core, T, topo):
         if n < NS:
             add += 32
         if n >= 1:
-            add += 16
+            add += 32
         if n == 1:
             add += 16
         cum[n % 2] += add
         g.wait_ge(G[n % 2], cum[n % 2])
         if acc:
             g.wait_ge(T.sem.acc, acc)
+        if 1 <= n and n + 1 < NS:
+            g.sem_inc(T.sem.go, 1)
+            for d in range(2):
+                lq[d].wait_ge(T.sem.go, n)
+            load(n + 1)
         if n < NS:
             h, H, s0, s1 = steps[n]
             trs = []
             for d in order:
-                dst = T.L[2 * (n % 3) + d]
+                dst = T.L[2 * (n % 4) + d]
                 if h == 1:
                     trs.append(RemoteDMATransfer(dst_ids=[ids[d]], dma_engine_mask=masks[d], remote_sem=G[(n + 1) % 2],
-                                                 src=T.S[d], dst=dst, alu_op=0))
+                                                 src=stage(n, d), dst=dst, alu_op=0))
                 else:
                     trs.append(RemoteDMATransfer(dst_ids=[ids[d]], dma_engine_mask=masks[d], remote_sem=G[(n + 1) % 2],
-                                                 srcs=[T.L[2 * ((n - 1) % 3) + d], T.S[d]], dsts=[dst], alu_op=1))
-            g.remote_dma_fused(trs, local_sem=T.sem.left)
-            if n + 1 < NS:
-                load(n + 1)
+                                                 srcs=[T.L[2 * ((n - 1) % 4) + d], stage(n, d)], dsts=[dst], alu_op=1))
+            g.remote_dma_fused(trs, local_sem=G[(n + 1) % 2])
         if n >= 1:
             h, H, s0, s1 = steps[n - 1]
             if h == H:
-                r = 2 * ((n - 1) % 3)
+                r = 2 * ((n - 1) % 4)
                 if s0 in (0, 1, 2, 4):
                     g.dma_start(piece(T.y, s0, 0, 2), T.L[r:r + 2], accum_op=AluOpType.add).then_inc(T.sem.acc, 16)
                     acc += 16
@@ -94,5 +98,4 @@ def rank_program(g, core, T, topo):
                     g.dma_start(piece(T.y, s0, 0), T.L[r], accum_op=AluOpType.add).then_inc(T.sem.acc, 16)
                     g.dma_start(piece(T.y, s1, 0), T.L[r + 1], accum_op=AluOpType.add).then_inc(T.sem.acc, 16)
                     acc += 32
-    g.wait_ge(T.sem.left, 16 * NS)
     g.wait_ge(T.sem.acc, acc)

@@ -16,7 +16,7 @@ def _plan():
     for k in range(NSL):
         H = 4 if k % 2 == 0 else 3
         for h in range(1, H + 1):
-            steps.append((h, H, k, (k + 1) % NSL))
+            steps.append((h, H, (k + 3) % NSL, (k + 4) % NSL))
     return steps
 
 
@@ -58,6 +58,7 @@ def rank_program(g, core, T, topo):
     g.scalar.dma_start(T.y[:, :], T.x[:, B * me:B * (me + 1)]).then_inc(G[1], 16)
 
     acc = 0
+    waited = 0
     for n in range(NS + 1):
         add = 0
         if n < NS:
@@ -68,13 +69,6 @@ def rank_program(g, core, T, topo):
             add += 16
         cum[n % 2] += add
         g.wait_ge(G[n % 2], cum[n % 2])
-        if acc:
-            g.wait_ge(T.sem.acc, acc)
-        if 1 <= n and n + 1 < NS:
-            g.sem_inc(T.sem.go, 1)
-            for d in range(2):
-                lq[d].wait_ge(T.sem.go, n)
-            load(n + 1)
         if n < NS:
             h, H, s0, s1 = steps[n]
             trs = []
@@ -87,6 +81,14 @@ def rank_program(g, core, T, topo):
                     trs.append(RemoteDMATransfer(dst_ids=[ids[d]], dma_engine_mask=masks[d], remote_sem=G[(n + 1) % 2],
                                                  srcs=[T.L[2 * ((n - 1) % 4) + d], stage(n, d)], dsts=[dst], alu_op=1))
             g.remote_dma_fused(trs, local_sem=G[(n + 1) % 2])
+        if acc > waited:
+            g.wait_ge(T.sem.acc, acc)
+            waited = acc
+        if 1 <= n and n + 1 < NS:
+            g.sem_inc(T.sem.go, 1)
+            for d in range(2):
+                lq[d].wait_ge(T.sem.go, n)
+            load(n + 1)
         if n >= 1:
             h, H, s0, s1 = steps[n - 1]
             if h == H:

from concourse.bass import DstId, RemoteDMATransfer
from concourse.mybir import AluOpType

RING = [1, 7, 47, 41, 121, 127, 87, 81]
NSL = 6
B = 48

SCRATCH = {
    "L": ("dram", [8, 128, 8], "float32"),
}
SEMAPHORES = ["G0", "G1", "go", "acc"]


def _plan():
    steps = []
    for k in range(NSL):
        H = 4 if k % 2 == 0 else 3
        for h in range(1, H + 1):
            steps.append((h, H, (k + 3) % NSL, (k + 4) % NSL))
    return steps


def rank_program(g, core, T, topo):
    if T.rank_of(core) is None:
        return
    p = RING.index(core)
    me = T.rank_of(core)
    steps = _plan()
    NS = len(steps)
    G = [T.sem.G0, T.sem.G1]
    cum = [0, 0]
    nbr = [RING[(p + 1) % 8], RING[(p - 1) % 8]]
    ids, masks = [], []
    for d in range(2):
        rid, pid, _se = topo.addr(nbr[d])
        ids.append(DstId(rid=rid, pnc=pid))
        masks.append(0xFF00 if topo.chip(nbr[d]) == topo.chip(core) else 0x00FF)
    order = [0, 1] if masks[0] == 0x00FF else [1, 0]
    lq = [g.sync, g.scalar]

    def piece(t, s, c0, m=1):
        if s < 4:
            return t[32 * s:32 * (s + m), c0:c0 + 32]
        return t[64 * (s - 4):64 * (s - 4 + m), c0 + 32:c0 + 48]

    def stage(n, d):
        return T.L[2 * ((n + 1) % 4) + (1 - d)]

    def load(n):
        h, H, s0, s1 = steps[n]
        for d in order:
            q = (p + (H - h + 1)) % 8 if d == 0 else (p - (H - h + 1)) % 8
            b = T.rank_of(RING[q])
            lq[d].dma_start(stage(n, d), piece(T.x, s0 if d == 0 else s1, B * b)).then_inc(G[n % 2], 16)

    load(0)
    load(1)
    g.scalar.dma_start(T.y[:, :], T.x[:, B * me:B * (me + 1)]).then_inc(G[1], 16)

    acc = 0
    waited = 0
    for n in range(NS + 1):
        add = 0
        if n < NS:
            add += 32
        if n >= 1:
            add += 32
        if n == 1:
            add += 16
        cum[n % 2] += add
        g.wait_ge(G[n % 2], cum[n % 2])
        if n < NS:
            h, H, s0, s1 = steps[n]
            trs = []
            for d in order:
                dst = T.L[2 * (n % 4) + d]
                if h == 1:
                    trs.append(RemoteDMATransfer(dst_ids=[ids[d]], dma_engine_mask=masks[d], remote_sem=G[(n + 1) % 2],
                                                 src=stage(n, d), dst=dst, alu_op=0))
                else:
                    trs.append(RemoteDMATransfer(dst_ids=[ids[d]], dma_engine_mask=masks[d], remote_sem=G[(n + 1) % 2],
                                                 srcs=[T.L[2 * ((n - 1) % 4) + d], stage(n, d)], dsts=[dst], alu_op=1))
            g.remote_dma_fused(trs, local_sem=G[(n + 1) % 2])
        if acc > waited:
            g.wait_ge(T.sem.acc, acc)
            waited = acc
        if 1 <= n and n + 1 < NS:
            g.sem_inc(T.sem.go, 1)
            for d in range(2):
                lq[d].wait_ge(T.sem.go, n)
            load(n + 1)
        if n >= 1:
            h, H, s0, s1 = steps[n - 1]
            if h == H:
                r = 2 * ((n - 1) % 4)
                if s0 in (0, 1, 2, 4):
                    g.dma_start(piece(T.y, s0, 0, 2), T.L[r:r + 2], accum_op=AluOpType.add).then_inc(T.sem.acc, 16)
                    acc += 16
                else:
                    g.dma_start(piece(T.y, s0, 0), T.L[r], accum_op=AluOpType.add).then_inc(T.sem.acc, 16)
                    g.dma_start(piece(T.y, s1, 0), T.L[r + 1], accum_op=AluOpType.add).then_inc(T.sem.acc, 16)
                    acc += 32
    g.wait_ge(T.sem.acc, acc)
